import numpy as np
import ml_dtypes


def mxq(x, axis, fmt="e4m3"):
    dtype, down = {"e4m3": (ml_dtypes.float8_e4m3fn, 7), "e5m2": (ml_dtypes.float8_e5m2, 14)}[fmt]
    v = np.moveaxis(np.asarray(x, np.float32).astype(ml_dtypes.bfloat16).astype(np.float64), axis, -1)
    blocks = v.reshape(v.shape[:-1] + (-1, 32))
    amax = np.abs(blocks).max(-1, keepdims=True)
    byte = np.maximum(np.where(amax > 0, np.frexp(amax)[1] - 1 + 127, 0) - down, 1)
    scale = np.exp2(byte - 127.0)
    codes = (blocks / scale).astype(np.float32).astype(dtype).astype(np.float64)
    return np.moveaxis((codes * scale).reshape(v.shape), -1, axis)


WIDE = False


def mx_kscale(k):
    if not WIDE:
        return np.ones(k)
    levels = np.array([10, -10, 5, -5, 0])
    if k % 512:
        return np.exp2(np.random.permutation(np.resize(levels, k // 32))).repeat(32)
    a = np.empty((k // 512, 16))
    for p in range(k // 512):
        a[p, :8] = np.random.permutation(np.resize(levels, 8))
        for g in range(8):
            far = levels[np.abs(levels - a[p, g]) >= 10]
            a[p, g + 8] = far[np.random.randint(len(far))]
    return np.exp2(a.ravel()).repeat(32)


def f64(x):
    return np.asarray(x).astype(np.float64)


def striped(idx):
    return np.tile(idx.reshape(-1, 16).T, (8, 1)).astype(np.uint16)


def unstriped(offs):
    return offs[:16].T.reshape(-1).astype(np.int64)


def pack_weight(w):
    k, n = w.shape
    w = f64(np.asarray(w, np.float32).astype(ml_dtypes.bfloat16)).reshape(k // 32, 32, n)
    amax = np.abs(w).max(1)
    byte = np.clip(np.where(amax > 0, np.frexp(amax)[1] - 1 + 127 - 7, 1), 1, 254)
    scaled = (w * np.exp2(127.0 - byte)[:, None, :]).reshape(k, n).astype(np.float32)
    words = np.ascontiguousarray(scaled.reshape(k // 512, 128, 4, n).transpose(0, 1, 3, 2)).astype(ml_dtypes.float8_e4m3fn).view(np.uint8)
    return words, np.ascontiguousarray(byte.astype(np.uint8).reshape(k // 512, 16, n))


def unpack_weight(words, scales):
    g, p, n, _ = words.shape
    vals = np.ascontiguousarray(words).view(ml_dtypes.float8_e4m3fn).astype(np.float64) * np.repeat(np.exp2(scales.astype(np.float64) - 127.0), 8, axis=1)[..., None]
    return vals.transpose(0, 1, 3, 2).reshape(g * 512, n)

def planes(y):
    n, m = y.shape
    v = y.astype(np.float32).astype(ml_dtypes.bfloat16).astype(np.float64).reshape(n // 32, 32, m)
    top = np.abs(v).max(1)
    byte = np.clip(np.where(top > 0, np.frexp(top)[1] - 1 + 127 - 7, 1), 1, 254)
    codes = (v * np.exp2(127.0 - byte)[:, None, :]).reshape(n, m).astype(np.float32).astype(ml_dtypes.float8_e4m3fn).view(np.uint8)
    words = codes.reshape(n // 512, 128, 4, m).transpose(0, 1, 3, 2)
    return np.ascontiguousarray(words), np.ascontiguousarray(byte.astype(np.uint8).reshape(n // 512, 16, m))


K, T, S, D, V, N = 512, 1024, 512, 4, 256, 512
P = 2 ** 7


def setup_inputs():
    n = np.random.standard_normal
    s = mx_kscale(K)[:, None]
    packed_xT = pack_weight(n((K, T)) * s)
    return {
        "x_words": packed_xT[0],
        "x_scales": packed_xT[1],
        "w1": (n((K, N)) / np.sqrt(K) / s).astype(np.float32),
        "score": np.tile(np.random.standard_normal((D, 1, V)), (1, P, 1)).astype(np.float32),
        "offs": striped(np.random.permutation(T)[:S]),
        "pos1": striped(np.random.permutation(S)[:V]),
        "pos2": striped(np.random.permutation(S)[:V]),
        "pos3": striped(np.random.permutation(S)[:V]),
        "pos4": striped(np.random.permutation(S)[:V]),
    }


def reference(x_words, x_scales, w1, score, offs, pos1, pos2, pos3, pos4):
    xq = unpack_weight(x_words, x_scales)[:, unstriped(offs)]
    y = mxq(f64(w1), 0, "e4m3").T @ xq
    e0 = np.exp(f64(score)[0, :1])
    e1 = np.exp(f64(score)[1, :1])
    e2 = np.exp(f64(score)[2, :1])
    e3 = np.exp(f64(score)[3, :1])
    num = y[:, unstriped(pos1)] * e0 + y[:, unstriped(pos2)] * e1 + y[:, unstriped(pos3)] * e2 + y[:, unstriped(pos4)] * e3
    den = e0 + e1 + e2 + e3
    out_0 = num / den
    return (out_0,) + planes(out_0)

@@ -1,0 +1,202 @@
+from contextlib import ExitStack
+
+import concourse.mybir as mybir
+
+K, T, S, D, V, N = 512, 1024, 512, 4, 256, 512
+P = 128
+FLOPS = 2 * K * N * S
+
+F32 = mybir.dt.float32
+BF16 = mybir.dt.bfloat16
+I32 = mybir.dt.int32
+U32 = mybir.dt.uint32
+U16 = mybir.dt.uint16
+U8 = mybir.dt.uint8
+FP8X4 = mybir.dt.float8_e4m3fn_x4
+ALU = mybir.AluOpType
+ACT = mybir.ActivationFunctionType
+AX = mybir.AxisListType
+
+FUSED = [0,0,1,1]
+W_COLS = [256,128,128]
+CAST_ENG = [[["s",64]],[["s",32]],[["v",20],["s",12]]]
+
+
+def tile_picked_gatv_none_po_kernel(
+    tc, x_words, x_scales, w1, score, offs, pos1, pos2, pos3, pos4, out_0, out_1, out_2
+):
+    nc = tc.nc
+    with ExitStack() as ctx:
+        lists = ctx.enter_context(tc.tile_pool(name="lists", bufs=1))
+        keep = ctx.enter_context(tc.tile_pool(name="keep", bufs=1))
+        ring = ctx.enter_context(tc.tile_pool(name="ring", bufs=8))
+        ps_f = ctx.enter_context(tc.psum_pool(name="ps_f", bufs=4))
+        ps_b = ctx.enter_context(tc.psum_pool(name="ps_b", bufs=4))
+
+        xs = keep.tile([P, T], U8, name="xs", align_bytes=64)
+        nc.vector.memset(xs[:].bitcast(I32), 0)
+        sc_raw = keep.tile([P, V], F32, name="sc_raw")
+        nc.vector.memset(sc_raw[:], 0.0)
+        ident = keep.tile([P, P], F32, name="ident")
+        ones = keep.tile([P, 32], F32, name="ones", align_bytes=64)
+        nc.vector.memset(ones[:], 1.0)
+        nc.vector.memset(ident[:], 0.0)
+        col = keep.tile([P, 32], F32, name="col", align_bytes=64)
+        nc.vector.tensor_tensor_scan(col[:], ones[:], ones[:], 0.0, ALU.mult, ALU.add)
+        row = keep.tile([P, 32], F32, name="row", align_bytes=64)
+        nc.vector.transpose(row[:], col[:])
+        for q in range(4):
+            part = slice(32 * q, 32 * q + 32)
+            nc.vector.tensor_tensor(ident[part, part], col[part, :], row[part, :], ALU.is_equal)
+
+        offs_t = lists.tile([P, S // 16], U16, name="offs_t")
+        nc.sync.dma_start(offs_t[:], offs)
+        xw = keep.tile([P, T], I32, name="xw", align_bytes=64)
+        nc.sync.dma_start(xw[:], x_words[0].rearrange("p c r -> p (c r)").bitcast(I32))
+        for q in range(4):
+            nc.sync.dma_start(xs[32 * q : 32 * q + 4, :].bitcast(I32), x_scales[0, 4 * q : 4 * q + 4, :].bitcast(I32))
+        w_rows = w1.rearrange("(p j) n -> p j n", j=4)
+        w_raw = []
+        c0 = 0
+        for c, cw in enumerate(W_COLS):
+            wt = keep.tile([P, 4, cw], F32, name="w_raw%d" % c)
+            nc.sync.dma_start(wt[:], w_rows[:, :, c0 : c0 + cw])
+            w_raw.append((wt, c0, cw))
+            c0 = c0 + cw
+        nc.sync.dma_start(sc_raw[0:P:32, :], score[:, 0, :])
+        pos_t = []
+        for d, pos in enumerate((pos1, pos2, pos3, pos4)):
+            pt = lists.tile([P, V // 16], U16, name="pos%d" % d)
+            nc.sync.dma_start(pt[:], pos)
+            pos_t.append(pt)
+
+        xs_g = keep.tile([P, S], U8, name="xs_g", align_bytes=64)
+        xw_g = keep.tile([P, S], U32, name="xw_g", align_bytes=64)
+        def gather_scales():
+            nc.vector.tensor_copy(xs_g[:], xs[:].indirect(offs_t[:]))
+        def gather_words():
+            for h in range(2):
+                nc.vector.tensor_copy(xw_g[:, h * 256 : (h + 1) * 256], xw[:].bitcast(U32).indirect(offs_t[:, h * 16 : (h + 1) * 16]))
+
+        wb = keep.tile([P, 4, P, 4], BF16, name="wb", align_bytes=64)
+        wq = keep.tile([P, N], U32, name="wq", align_bytes=64)
+        wsc = keep.tile([P, N], U8, name="wsc", align_bytes=64)
+        def cast_w():
+            for c, (wt, c0, cw) in enumerate(w_raw):
+                parts = CAST_ENG[c]
+                m0 = 0
+                for eng, mw in parts:
+                    dst = wb[:, :, c0 // 4 + m0 : c0 // 4 + m0 + mw, :].rearrange("p t m j -> p m j t")
+                    src = wt[:, :, 4 * m0 : 4 * (m0 + mw)].rearrange("p j (m t) -> p m j t", t=4)
+                    if eng == "s":
+                        nc.scalar.activation(dst, src, ACT.Copy)
+                    else:
+                        nc.vector.tensor_copy(dst, src)
+                    m0 = m0 + mw
+        def quant_w():
+            for t in range(4):
+                nc.vector.quantize_mx(wq[:, t * P : (t + 1) * P].bitcast(FP8X4), wsc[:, t * P : (t + 1) * P], wb[:, t, :, :].rearrange("p m j -> p (m j)"))
+        gather_words()
+        gather_scales()
+        cast_w()
+        quant_w()
+
+        y = []
+        for t in range(4):
+            yt = keep.tile([P, S], F32, name="y%d" % t)
+            pieces = [(0, 256), (256, 512)] if t == 0 else [(0, 512)]
+            for i, (s0, s1) in enumerate(pieces):
+                acc = ps_b.tile([P, 512], F32, name="back")
+                nc.tensor.matmul_mx(acc[:, 0 : s1 - s0], wq[:, t * P : (t + 1) * P].bitcast(FP8X4), wsc[:, t * P : (t + 1) * P],
+                                    xw_g[:, s0:s1].bitcast(FP8X4), xs_g[:, s0:s1], start=True, stop=True)
+                if t == 0 and i == 0:
+                    nc.vector.tensor_copy(yt[:, s0:s1], acc[:, 0 : s1 - s0])
+                else:
+                    nc.scalar.copy(yt[:, s0:s1], acc[:, 0 : s1 - s0])
+            y.append(yt)
+
+        sc_ps = ps_f.tile([P, 2, P], F32, name="f")
+        for h in range(2):
+            nc.tensor.transpose(sc_ps[:, h, :], sc_raw[:, h * P : (h + 1) * P], ident[:])
+        sc_v = sc_ps[:, :, 0:P:32]
+        ntop = keep.tile([P, 2], F32, name="ntop")
+        nc.vector.tensor_reduce(ntop[:], sc_v, AX.X, ALU.max, negate=True)
+        e = keep.tile([P, 2, D], F32, name="e")
+        den = keep.tile([P, 2], F32, name="den")
+        for h in range(2):
+            nc.scalar.activation(e[:, h, :], sc_v[:, h, :], ACT.Exp, bias=ntop[:, h : h + 1], accum_out=den[:, h : h + 1])
+        inv = keep.tile([P, 2], F32, name="inv")
+        nc.vector.reciprocal(inv[:], den[:])
+        a = keep.tile([P, 2, D], F32, name="a")
+        nc.vector.tensor_tensor(a[:], e[:], inv[:].unsqueeze(2).to_broadcast([P, 2, D]), ALU.mult)
+
+        a_row = {}
+        nf = max(FUSED)
+        for d0 in range(D - nf, D, 2):
+            ds = list(range(d0, min(d0 + 2, D)))
+            bc = ps_f.tile([P, 2, 2, P], F32, name="f")
+            for i, d in enumerate(ds):
+                for h in range(2):
+                    nc.tensor.transpose(bc[:, i, h, :], a[:, h, d : d + 1].to_broadcast([P, P]), ident[:])
+            ar = keep.tile([P, len(ds), V], F32, name="a_row%d" % d0)
+            nc.scalar.copy(ar[:], bc[:, 0 : len(ds), :, :].rearrange("p i h v -> p i (h v)"))
+            for i, d in enumerate(ds):
+                a_row[d] = ar[:, i, :]
+
+        o = keep.tile([P, 4, V], F32, name="o")
+        out_rows = out_0.rearrange("(p t) v -> p t v", t=4)
+        back = {}
+        prod = {}
+
+        def plain_part(t):
+            nplain = D - FUSED[t]
+            b = [ps_b.tile([P, P], F32, name="back") for h in range(2)]
+            for d in range(nplain):
+                g = ring.tile([P, V], F32, name="g")
+                nc.vector.tensor_copy(g[:], y[t][:].indirect(pos_t[d][:]))
+                f = ps_f.tile([P, 2, P], F32, name="f")
+                for h in range(2):
+                    nc.tensor.transpose(f[:, h, :], g[:, h * P : (h + 1) * P], ident[:])
+                sc = ring.tile([P, 2, P], F32, name="sc")
+                for h in range(2):
+                    nc.scalar.activation(sc[:, h, :], f[:, h, :], ACT.Copy, scale=a[:, h, d : d + 1])
+                for h in range(2):
+                    nc.tensor.matmul(b[h][:], sc[:, h, :], ident[:], start=(d == 0), stop=(d == nplain - 1), is_transpose=True)
+            back[t] = b
+            if FUSED[t] == 0:
+                for h in range(2):
+                    nc.scalar.copy(o[:, t, h * P : (h + 1) * P], b[h][:])
+                nc.sync.dma_start(out_rows[:, t, :], o[:, t, :])
+
+        def fused_part(t):
+            for d in range(D - FUSED[t], D):
+                c = ring.tile([P, V], F32, name="g")
+                nc.vector.tensor_tensor(c[:], y[t][:].indirect(pos_t[d][:]), a_row[d], ALU.mult)
+                prod[(t, d)] = c
+
+        def finish(t):
+            for h in range(2):
+                cols = slice(h * P, (h + 1) * P)
+                nc.vector.tensor_tensor(o[:, t, cols], back[t][h][:], prod[(t, D - 1)][:, cols], ALU.add)
+            nc.sync.dma_start(out_rows[:, t, :], o[:, t, :])
+
+        for step in ["p0","p1","p2","p3","c2","c3","f2","f3"]:
+            kind, t = step[0], int(step[1])
+            if kind == "p":
+                plain_part(t)
+            elif kind == "c":
+                fused_part(t)
+            else:
+                finish(t)
+
+        ob = keep.tile([P, V, 4], BF16, name="ob", align_bytes=64)
+        SPLIT = 160
+        nc.vector.tensor_copy(ob[:, 0:SPLIT, :].rearrange("p (c i) t -> p c t i", i=4), o[:, :, 0:SPLIT].rearrange("p t (c i) -> p c t i", i=4))
+        nc.scalar.copy(ob[:, SPLIT:V, :].rearrange("p (c i) t -> p c t i", i=4), o[:, :, SPLIT:V].rearrange("p t (c i) -> p c t i", i=4))
+        oq = keep.tile([P, V], U32, name="oq", align_bytes=64)
+        osc = keep.tile([P, V], U8, name="osc", align_bytes=64)
+        nc.vector.quantize_mx(oq[:].bitcast(FP8X4), osc[:], ob[:].rearrange("p v t -> p (v t)"))
+        nc.sync.dma_start(out_1[0].rearrange("p c r -> p (c r)").bitcast(I32), oq[:].bitcast(I32))
+        for q in range(4):
+            eng = nc.scalar if q < 2 else nc.sync
+            eng.dma_start(out_2[0, 4 * q : 4 * q + 4, :].bitcast(I32), osc[32 * q : 32 * q + 4, :].bitcast(I32))

@@ -17,9 +17,9 @@ ALU = mybir.AluOpType
 ACT = mybir.ActivationFunctionType
 AX = mybir.AxisListType
 
-FUSED = [0,0,1,1]
-W_COLS = [256,128,128]
-CAST_ENG = [[["s",64]],[["s",32]],[["v",20],["s",12]]]
+FUSED = [1,1,1,1]
+W_COLS = [256,256]
+CAST_ENG = [[["s",64]],[["v",40],["s",24]]]
 
 
 def tile_picked_gatv_none_po_kernel(
@@ -93,28 +93,13 @@ def tile_picked_gatv_none_po_kernel(
                     else:
                         nc.vector.tensor_copy(dst, src)
                     m0 = m0 + mw
-        def quant_w():
-            for t in range(4):
+        def quant_w(ts):
+            for t in ts:
                 nc.vector.quantize_mx(wq[:, t * P : (t + 1) * P].bitcast(FP8X4), wsc[:, t * P : (t + 1) * P], wb[:, t, :, :].rearrange("p m j -> p (m j)"))
         gather_words()
         gather_scales()
         cast_w()
-        quant_w()
-
-        y = []
-        for t in range(4):
-            yt = keep.tile([P, S], F32, name="y%d" % t)
-            pieces = [(0, 256), (256, 512)] if t == 0 else [(0, 512)]
-            for i, (s0, s1) in enumerate(pieces):
-                acc = ps_b.tile([P, 512], F32, name="back")
-                nc.tensor.matmul_mx(acc[:, 0 : s1 - s0], wq[:, t * P : (t + 1) * P].bitcast(FP8X4), wsc[:, t * P : (t + 1) * P],
-                                    xw_g[:, s0:s1].bitcast(FP8X4), xs_g[:, s0:s1], start=True, stop=True)
-                if t == 0 and i == 0:
-                    nc.vector.tensor_copy(yt[:, s0:s1], acc[:, 0 : s1 - s0])
-                else:
-                    nc.scalar.copy(yt[:, s0:s1], acc[:, 0 : s1 - s0])
-            y.append(yt)
-
+        quant_w([0])
         sc_ps = ps_f.tile([P, 2, P], F32, name="f")
         for h in range(2):
             nc.tensor.transpose(sc_ps[:, h, :], sc_raw[:, h * P : (h + 1) * P], ident[:])
@@ -129,6 +114,22 @@ def tile_picked_gatv_none_po_kernel(
         nc.vector.reciprocal(inv[:], den[:])
         a = keep.tile([P, 2, D], F32, name="a")
         nc.vector.tensor_tensor(a[:], e[:], inv[:].unsqueeze(2).to_broadcast([P, 2, D]), ALU.mult)
+
+        quant_w([1, 2, 3])
+
+        y = []
+        for t in range(4):
+            yt = keep.tile([P, S], F32, name="y%d" % t)
+            pieces = [(0, 256), (256, 512)] if t == 0 else [(0, 512)]
+            for i, (s0, s1) in enumerate(pieces):
+                acc = ps_b.tile([P, 512], F32, name="back")
+                nc.tensor.matmul_mx(acc[:, 0 : s1 - s0], wq[:, t * P : (t + 1) * P].bitcast(FP8X4), wsc[:, t * P : (t + 1) * P],
+                                    xw_g[:, s0:s1].bitcast(FP8X4), xs_g[:, s0:s1], start=True, stop=True)
+                if t == 0 and i == 0:
+                    nc.vector.tensor_copy(yt[:, s0:s1], acc[:, 0 : s1 - s0])
+                else:
+                    nc.scalar.copy(yt[:, s0:s1], acc[:, 0 : s1 - s0])
+            y.append(yt)
 
         a_row = {}
         nf = max(FUSED)
@@ -174,28 +175,29 @@ def tile_picked_gatv_none_po_kernel(
                 nc.vector.tensor_tensor(c[:], y[t][:].indirect(pos_t[d][:]), a_row[d], ALU.mult)
                 prod[(t, d)] = c
 
-        def finish(t):
-            for h in range(2):
-                cols = slice(h * P, (h + 1) * P)
-                nc.vector.tensor_tensor(o[:, t, cols], back[t][h][:], prod[(t, D - 1)][:, cols], ALU.add)
-            nc.sync.dma_start(out_rows[:, t, :], o[:, t, :])
+        def finish(t, h):
+            cols = slice(h * P, (h + 1) * P)
+            nc.vector.tensor_tensor(o[:, t, cols], back[t][h][:], prod[(t, D - 1)][:, cols], ALU.add)
+            if h == 1:
+                nc.sync.dma_start(out_rows[:, t, :], o[:, t, :])
 
-        for step in ["p0","p1","p2","p3","c2","c3","f2","f3"]:
+        for step in ["p0","c0","p1","c1","f00","f01","p2","f10","f11","p3","c2","c3","f20","f30","f21","f31"]:
             kind, t = step[0], int(step[1])
             if kind == "p":
                 plain_part(t)
             elif kind == "c":
                 fused_part(t)
             else:
-                finish(t)
+                finish(t, int(step[2]))
 
         ob = keep.tile([P, V, 4], BF16, name="ob", align_bytes=64)
-        SPLIT = 160
-        nc.vector.tensor_copy(ob[:, 0:SPLIT, :].rearrange("p (c i) t -> p c t i", i=4), o[:, :, 0:SPLIT].rearrange("p t (c i) -> p c t i", i=4))
-        nc.scalar.copy(ob[:, SPLIT:V, :].rearrange("p (c i) t -> p c t i", i=4), o[:, :, SPLIT:V].rearrange("p t (c i) -> p c t i", i=4))
         oq = keep.tile([P, V], U32, name="oq", align_bytes=64)
         osc = keep.tile([P, V], U8, name="osc", align_bytes=64)
-        nc.vector.quantize_mx(oq[:].bitcast(FP8X4), osc[:], ob[:].rearrange("p v t -> p (v t)"))
+        nc.scalar.copy(ob[:, 0:P, :].rearrange("p (c i) t -> p c t i", i=4), o[:, :, 0:P].rearrange("p t (c i) -> p c t i", i=4))
+        nc.vector.tensor_copy(ob[:, P:V, :].rearrange("p (c i) t -> p c t i", i=4), o[:, :, P:V].rearrange("p t (c i) -> p c t i", i=4))
+        for h in range(2):
+            cols = slice(h * P, (h + 1) * P)
+            nc.vector.quantize_mx(oq[:, cols].bitcast(FP8X4), osc[:, cols], ob[:, cols, :].rearrange("p v t -> p (v t)"))
         nc.sync.dma_start(out_1[0].rearrange("p c r -> p (c r)").bitcast(I32), oq[:].bitcast(I32))
         for q in range(4):
             eng = nc.scalar if q < 2 else nc.sync

@@ -17,7 +17,8 @@ ALU = mybir.AluOpType
 ACT = mybir.ActivationFunctionType
 AX = mybir.AxisListType
 
-FUSED = [1,1,1,1]
+FUSED = [0,1,1,1]
+PIECES = [(0, 256), (256, 384), (384, 512)]
 W_COLS = [256,256]
 CAST_ENG = [[["s",64]],[["v",40],["s",24]]]
 
@@ -51,10 +52,6 @@ def tile_picked_gatv_none_po_kernel(
 
         offs_t = lists.tile([P, S // 16], U16, name="offs_t")
         nc.sync.dma_start(offs_t[:], offs)
-        xw = keep.tile([P, T], I32, name="xw", align_bytes=64)
-        nc.sync.dma_start(xw[:], x_words[0].rearrange("p c r -> p (c r)").bitcast(I32))
-        for q in range(4):
-            nc.sync.dma_start(xs[32 * q : 32 * q + 4, :].bitcast(I32), x_scales[0, 4 * q : 4 * q + 4, :].bitcast(I32))
         w_rows = w1.rearrange("(p j) n -> p j n", j=4)
         w_raw = []
         c0 = 0
@@ -62,8 +59,13 @@ def tile_picked_gatv_none_po_kernel(
             wt = keep.tile([P, 4, cw], F32, name="w_raw%d" % c)
             nc.sync.dma_start(wt[:], w_rows[:, :, c0 : c0 + cw])
             w_raw.append((wt, c0, cw))
+            if c == 0:
+                for q in range(4):
+                    nc.sync.dma_start(xs[32 * q : 32 * q + 4, :].bitcast(I32), x_scales[0, 4 * q : 4 * q + 4, :].bitcast(I32))
             c0 = c0 + cw
         nc.sync.dma_start(sc_raw[0:P:32, :], score[:, 0, :])
+        xw = keep.tile([P, T], I32, name="xw", align_bytes=64)
+        nc.sync.dma_start(xw[:], x_words[0].rearrange("p c r -> p (c r)").bitcast(I32))
         pos_t = []
         for d, pos in enumerate((pos1, pos2, pos3, pos4)):
             pt = lists.tile([P, V // 16], U16, name="pos%d" % d)
@@ -75,11 +77,11 @@ def tile_picked_gatv_none_po_kernel(
         def gather_scales():
             nc.vector.tensor_copy(xs_g[:], xs[:].indirect(offs_t[:]))
         def gather_words():
-            for h in range(2):
-                nc.vector.tensor_copy(xw_g[:, h * 256 : (h + 1) * 256], xw[:].bitcast(U32).indirect(offs_t[:, h * 16 : (h + 1) * 16]))
+            for s0, s1 in PIECES:
+                nc.vector.tensor_copy(xw_g[:, s0:s1], xw[:].bitcast(U32).indirect(offs_t[:, s0 // 16 : s1 // 16]))
 
         wb = keep.tile([P, 4, P, 4], BF16, name="wb", align_bytes=64)
-        wq = keep.tile([P, N], U32, name="wq", align_bytes=64)
+        wq = {0: keep.tile([P, P], U32, name="wq", align_bytes=64)[:]}
         wsc = keep.tile([P, N], U8, name="wsc", align_bytes=64)
         def cast_w():
             for c, (wt, c0, cw) in enumerate(w_raw):
@@ -95,11 +97,11 @@ def tile_picked_gatv_none_po_kernel(
                     m0 = m0 + mw
         def quant_w(ts):
             for t in ts:
-                nc.vector.quantize_mx(wq[:, t * P : (t + 1) * P].bitcast(FP8X4), wsc[:, t * P : (t + 1) * P], wb[:, t, :, :].rearrange("p m j -> p (m j)"))
-        gather_words()
+                nc.vector.quantize_mx(wq[t].bitcast(FP8X4), wsc[:, t * P : (t + 1) * P], wb[:, t, :, :].rearrange("p m j -> p (m j)"))
         gather_scales()
         cast_w()
         quant_w([0])
+        gather_words()
         sc_ps = ps_f.tile([P, 2, P], F32, name="f")
         for h in range(2):
             nc.tensor.transpose(sc_ps[:, h, :], sc_raw[:, h * P : (h + 1) * P], ident[:])
@@ -110,22 +112,25 @@ def tile_picked_gatv_none_po_kernel(
         den = keep.tile([P, 2], F32, name="den")
         for h in range(2):
             nc.scalar.activation(e[:, h, :], sc_v[:, h, :], ACT.Exp, bias=ntop[:, h : h + 1], accum_out=den[:, h : h + 1])
-        inv = keep.tile([P, 2], F32, name="inv")
+        inv = keep.tile([P, 2], F32, name="xw", align_bytes=64)
         nc.vector.reciprocal(inv[:], den[:])
         a = keep.tile([P, 2, D], F32, name="a")
         nc.vector.tensor_tensor(a[:], e[:], inv[:].unsqueeze(2).to_broadcast([P, 2, D]), ALU.mult)
 
+        rest = keep.tile([P, 3 * P], U32, name="xw", align_bytes=64)
+        for t in (1, 2, 3):
+            wq[t] = rest[:, (t - 1) * P : t * P]
         quant_w([1, 2, 3])
 
         y = []
         for t in range(4):
             yt = keep.tile([P, S], F32, name="y%d" % t)
-            pieces = [(0, 256), (256, 512)] if t == 0 else [(0, 512)]
+            pieces = PIECES if t == 0 else [(0, 512)]
             for i, (s0, s1) in enumerate(pieces):
                 acc = ps_b.tile([P, 512], F32, name="back")
-                nc.tensor.matmul_mx(acc[:, 0 : s1 - s0], wq[:, t * P : (t + 1) * P].bitcast(FP8X4), wsc[:, t * P : (t + 1) * P],
+                nc.tensor.matmul_mx(acc[:, 0 : s1 - s0], wq[t].bitcast(FP8X4), wsc[:, t * P : (t + 1) * P],
                                     xw_g[:, s0:s1].bitcast(FP8X4), xs_g[:, s0:s1], start=True, stop=True)
-                if t == 0 and i == 0:
+                if t == 0 and i == -1:
                     nc.vector.tensor_copy(yt[:, s0:s1], acc[:, 0 : s1 - s0])
                 else:
                     nc.scalar.copy(yt[:, s0:s1], acc[:, 0 : s1 - s0])
@@ -151,7 +156,7 @@ def tile_picked_gatv_none_po_kernel(
 
         def plain_part(t):
             nplain = D - FUSED[t]
-            b = [ps_b.tile([P, P], F32, name="back") for h in range(2)]
+            scaled = []
             for d in range(nplain):
                 g = ring.tile([P, V], F32, name="g")
                 nc.vector.tensor_copy(g[:], y[t][:].indirect(pos_t[d][:]))
@@ -161,12 +166,14 @@ def tile_picked_gatv_none_po_kernel(
                 sc = ring.tile([P, 2, P], F32, name="sc")
                 for h in range(2):
                     nc.scalar.activation(sc[:, h, :], f[:, h, :], ACT.Copy, scale=a[:, h, d : d + 1])
-                for h in range(2):
-                    nc.tensor.matmul(b[h][:], sc[:, h, :], ident[:], start=(d == 0), stop=(d == nplain - 1), is_transpose=True)
+                scaled.append(sc)
+            b = ps_b.tile([P, V], F32, name="back")
+            for h in range(2):
+                for d in range(nplain):
+                    nc.tensor.matmul(b[:, h * P : (h + 1) * P], scaled[d][:, h, :], ident[:], start=(d == 0), stop=(d == nplain - 1), is_transpose=True)
             back[t] = b
             if FUSED[t] == 0:
-                for h in range(2):
-                    nc.scalar.copy(o[:, t, h * P : (h + 1) * P], b[h][:])
+                nc.scalar.copy(o[:, t, :], b[:])
                 nc.sync.dma_start(out_rows[:, t, :], o[:, t, :])
 
         def fused_part(t):
@@ -176,12 +183,12 @@ def tile_picked_gatv_none_po_kernel(
                 prod[(t, d)] = c
 
         def finish(t, h):
-            cols = slice(h * P, (h + 1) * P)
-            nc.vector.tensor_tensor(o[:, t, cols], back[t][h][:], prod[(t, D - 1)][:, cols], ALU.add)
-            if h == 1:
+            cols = slice(h * P, (h + 1) * P) if h < 2 else slice(0, V)
+            nc.vector.tensor_tensor(o[:, t, cols], back[t][:, cols], prod[(t, D - 1)][:, cols], ALU.add)
+            if h >= 1:
                 nc.sync.dma_start(out_rows[:, t, :], o[:, t, :])
 
-        for step in ["p0","c0","p1","c1","f00","f01","p2","f10","f11","p3","c2","c3","f20","f30","f21","f31"]:
+        for step in ["p0","p1","p2","p3","c1","c2","f12","c3","f22","f30","f31"]:
             kind, t = step[0], int(step[1])
             if kind == "p":
                 plain_part(t)

from contextlib import ExitStack

import concourse.mybir as mybir

K, T, S, D, V, N = 512, 1024, 512, 4, 256, 512
P = 128
FLOPS = 2 * K * N * S

F32 = mybir.dt.float32
BF16 = mybir.dt.bfloat16
I32 = mybir.dt.int32
U32 = mybir.dt.uint32
U16 = mybir.dt.uint16
U8 = mybir.dt.uint8
FP8X4 = mybir.dt.float8_e4m3fn_x4
ALU = mybir.AluOpType
ACT = mybir.ActivationFunctionType
AX = mybir.AxisListType

FUSED = [0,1,1,1]
PIECES = [(0, 256), (256, 384), (384, 512)]
W_COLS = [256,256]
CAST_ENG = [[["s",64]],[["v",40],["s",24]]]


def tile_picked_gatv_none_po_kernel(
    tc, x_words, x_scales, w1, score, offs, pos1, pos2, pos3, pos4, out_0, out_1, out_2
):
    nc = tc.nc
    with ExitStack() as ctx:
        lists = ctx.enter_context(tc.tile_pool(name="lists", bufs=1))
        keep = ctx.enter_context(tc.tile_pool(name="keep", bufs=1))
        ring = ctx.enter_context(tc.tile_pool(name="ring", bufs=8))
        ps_f = ctx.enter_context(tc.psum_pool(name="ps_f", bufs=4))
        ps_b = ctx.enter_context(tc.psum_pool(name="ps_b", bufs=4))

        xs = keep.tile([P, T], U8, name="xs", align_bytes=64)
        nc.vector.memset(xs[:].bitcast(I32), 0)
        sc_raw = keep.tile([P, V], F32, name="sc_raw")
        nc.vector.memset(sc_raw[:], 0.0)
        ident = keep.tile([P, P], F32, name="ident")
        ones = keep.tile([P, 32], F32, name="ones", align_bytes=64)
        nc.vector.memset(ones[:], 1.0)
        nc.vector.memset(ident[:], 0.0)
        col = keep.tile([P, 32], F32, name="col", align_bytes=64)
        nc.vector.tensor_tensor_scan(col[:], ones[:], ones[:], 0.0, ALU.mult, ALU.add)
        row = keep.tile([P, 32], F32, name="row", align_bytes=64)
        nc.vector.transpose(row[:], col[:])
        for q in range(4):
            part = slice(32 * q, 32 * q + 32)
            nc.vector.tensor_tensor(ident[part, part], col[part, :], row[part, :], ALU.is_equal)

        offs_t = lists.tile([P, S // 16], U16, name="offs_t")
        nc.sync.dma_start(offs_t[:], offs)
        w_rows = w1.rearrange("(p j) n -> p j n", j=4)
        w_raw = []
        c0 = 0
        for c, cw in enumerate(W_COLS):
            wt = keep.tile([P, 4, cw], F32, name="w_raw%d" % c)
            nc.sync.dma_start(wt[:], w_rows[:, :, c0 : c0 + cw])
            w_raw.append((wt, c0, cw))
            if c == 0:
                for q in range(4):
                    nc.sync.dma_start(xs[32 * q : 32 * q + 4, :].bitcast(I32), x_scales[0, 4 * q : 4 * q + 4, :].bitcast(I32))
            c0 = c0 + cw
        nc.sync.dma_start(sc_raw[0:P:32, :], score[:, 0, :])
        xw = keep.tile([P, T], I32, name="xw", align_bytes=64)
        nc.sync.dma_start(xw[:], x_words[0].rearrange("p c r -> p (c r)").bitcast(I32))
        pos_t = []
        for d, pos in enumerate((pos1, pos2, pos3, pos4)):
            pt = lists.tile([P, V // 16], U16, name="pos%d" % d)
            nc.sync.dma_start(pt[:], pos)
            pos_t.append(pt)

        xs_g = keep.tile([P, S], U8, name="xs_g", align_bytes=64)
        xw_g = keep.tile([P, S], U32, name="xw_g", align_bytes=64)
        def gather_scales():
            nc.vector.tensor_copy(xs_g[:], xs[:].indirect(offs_t[:]))
        def gather_words():
            for s0, s1 in PIECES:
                nc.vector.tensor_copy(xw_g[:, s0:s1], xw[:].bitcast(U32).indirect(offs_t[:, s0 // 16 : s1 // 16]))

        wb = keep.tile([P, 4, P, 4], BF16, name="wb", align_bytes=64)
        wq = {0: keep.tile([P, P], U32, name="wq", align_bytes=64)[:]}
        wsc = keep.tile([P, N], U8, name="wsc", align_bytes=64)
        def cast_w():
            for c, (wt, c0, cw) in enumerate(w_raw):
                parts = CAST_ENG[c]
                m0 = 0
                for eng, mw in parts:
                    dst = wb[:, :, c0 // 4 + m0 : c0 // 4 + m0 + mw, :].rearrange("p t m j -> p m j t")
                    src = wt[:, :, 4 * m0 : 4 * (m0 + mw)].rearrange("p j (m t) -> p m j t", t=4)
                    if eng == "s":
                        nc.scalar.activation(dst, src, ACT.Copy)
                    else:
                        nc.vector.tensor_copy(dst, src)
                    m0 = m0 + mw
        def quant_w(ts):
            for t in ts:
                nc.vector.quantize_mx(wq[t].bitcast(FP8X4), wsc[:, t * P : (t + 1) * P], wb[:, t, :, :].rearrange("p m j -> p (m j)"))
        gather_scales()
        cast_w()
        quant_w([0])
        gather_words()
        sc_ps = ps_f.tile([P, 2, P], F32, name="f")
        for h in range(2):
            nc.tensor.transpose(sc_ps[:, h, :], sc_raw[:, h * P : (h + 1) * P], ident[:])
        sc_v = sc_ps[:, :, 0:P:32]
        ntop = keep.tile([P, 2], F32, name="ntop")
        nc.vector.tensor_reduce(ntop[:], sc_v, AX.X, ALU.max, negate=True)
        e = keep.tile([P, 2, D], F32, name="e")
        den = keep.tile([P, 2], F32, name="den")
        for h in range(2):
            nc.scalar.activation(e[:, h, :], sc_v[:, h, :], ACT.Exp, bias=ntop[:, h : h + 1], accum_out=den[:, h : h + 1])
        inv = keep.tile([P, 2], F32, name="xw", align_bytes=64)
        nc.vector.reciprocal(inv[:], den[:])
        a = keep.tile([P, 2, D], F32, name="a")
        nc.vector.tensor_tensor(a[:], e[:], inv[:].unsqueeze(2).to_broadcast([P, 2, D]), ALU.mult)

        rest = keep.tile([P, 3 * P], U32, name="xw", align_bytes=64)
        for t in (1, 2, 3):
            wq[t] = rest[:, (t - 1) * P : t * P]
        quant_w([1, 2, 3])

        y = []
        for t in range(4):
            yt = keep.tile([P, S], F32, name="y%d" % t)
            pieces = PIECES if t == 0 else [(0, 512)]
            for i, (s0, s1) in enumerate(pieces):
                acc = ps_b.tile([P, 512], F32, name="back")
                nc.tensor.matmul_mx(acc[:, 0 : s1 - s0], wq[t].bitcast(FP8X4), wsc[:, t * P : (t + 1) * P],
                                    xw_g[:, s0:s1].bitcast(FP8X4), xs_g[:, s0:s1], start=True, stop=True)
                if t == 0 and i == -1:
                    nc.vector.tensor_copy(yt[:, s0:s1], acc[:, 0 : s1 - s0])
                else:
                    nc.scalar.copy(yt[:, s0:s1], acc[:, 0 : s1 - s0])
            y.append(yt)

        a_row = {}
        nf = max(FUSED)
        for d0 in range(D - nf, D, 2):
            ds = list(range(d0, min(d0 + 2, D)))
            bc = ps_f.tile([P, 2, 2, P], F32, name="f")
            for i, d in enumerate(ds):
                for h in range(2):
                    nc.tensor.transpose(bc[:, i, h, :], a[:, h, d : d + 1].to_broadcast([P, P]), ident[:])
            ar = keep.tile([P, len(ds), V], F32, name="a_row%d" % d0)
            nc.scalar.copy(ar[:], bc[:, 0 : len(ds), :, :].rearrange("p i h v -> p i (h v)"))
            for i, d in enumerate(ds):
                a_row[d] = ar[:, i, :]

        o = keep.tile([P, 4, V], F32, name="o")
        out_rows = out_0.rearrange("(p t) v -> p t v", t=4)
        back = {}
        prod = {}

        def plain_part(t):
            nplain = D - FUSED[t]
            scaled = []
            for d in range(nplain):
                g = ring.tile([P, V], F32, name="g")
                nc.vector.tensor_copy(g[:], y[t][:].indirect(pos_t[d][:]))
                f = ps_f.tile([P, 2, P], F32, name="f")
                for h in range(2):
                    nc.tensor.transpose(f[:, h, :], g[:, h * P : (h + 1) * P], ident[:])
                sc = ring.tile([P, 2, P], F32, name="sc")
                for h in range(2):
                    nc.scalar.activation(sc[:, h, :], f[:, h, :], ACT.Copy, scale=a[:, h, d : d + 1])
                scaled.append(sc)
            b = ps_b.tile([P, V], F32, name="back")
            for h in range(2):
                for d in range(nplain):
                    nc.tensor.matmul(b[:, h * P : (h + 1) * P], scaled[d][:, h, :], ident[:], start=(d == 0), stop=(d == nplain - 1), is_transpose=True)
            back[t] = b
            if FUSED[t] == 0:
                nc.scalar.copy(o[:, t, :], b[:])
                nc.sync.dma_start(out_rows[:, t, :], o[:, t, :])

        def fused_part(t):
            for d in range(D - FUSED[t], D):
                c = ring.tile([P, V], F32, name="g")
                nc.vector.tensor_tensor(c[:], y[t][:].indirect(pos_t[d][:]), a_row[d], ALU.mult)
                prod[(t, d)] = c

        def finish(t, h):
            cols = slice(h * P, (h + 1) * P) if h < 2 else slice(0, V)
            nc.vector.tensor_tensor(o[:, t, cols], back[t][:, cols], prod[(t, D - 1)][:, cols], ALU.add)
            if h >= 1:
                nc.sync.dma_start(out_rows[:, t, :], o[:, t, :])

        for step in ["p0","p1","p2","p3","c1","c2","f12","c3","f22","f30","f31"]:
            kind, t = step[0], int(step[1])
            if kind == "p":
                plain_part(t)
            elif kind == "c":
                fused_part(t)
            else:
                finish(t, int(step[2]))

        ob = keep.tile([P, V, 4], BF16, name="ob", align_bytes=64)
        oq = keep.tile([P, V], U32, name="oq", align_bytes=64)
        osc = keep.tile([P, V], U8, name="osc", align_bytes=64)
        nc.scalar.copy(ob[:, 0:P, :].rearrange("p (c i) t -> p c t i", i=4), o[:, :, 0:P].rearrange("p t (c i) -> p c t i", i=4))
        nc.vector.tensor_copy(ob[:, P:V, :].rearrange("p (c i) t -> p c t i", i=4), o[:, :, P:V].rearrange("p t (c i) -> p c t i", i=4))
        for h in range(2):
            cols = slice(h * P, (h + 1) * P)
            nc.vector.quantize_mx(oq[:, cols].bitcast(FP8X4), osc[:, cols], ob[:, cols, :].rearrange("p v t -> p (v t)"))
        nc.sync.dma_start(out_1[0].rearrange("p c r -> p (c r)").bitcast(I32), oq[:].bitcast(I32))
        for q in range(4):
            eng = nc.scalar if q < 2 else nc.sync
            eng.dma_start(out_2[0, 4 * q : 4 * q + 4, :].bitcast(I32), osc[32 * q : 32 * q + 4, :].bitcast(I32))
